import numpy as np
import ml_dtypes


def mxq(x, axis, fmt="e4m3"):
    dtype, down = {"e4m3": (ml_dtypes.float8_e4m3fn, 7), "e5m2": (ml_dtypes.float8_e5m2, 14)}[fmt]
    v = np.moveaxis(np.asarray(x, np.float32).astype(ml_dtypes.bfloat16).astype(np.float64), axis, -1)
    blocks = v.reshape(v.shape[:-1] + (-1, 32))
    amax = np.abs(blocks).max(-1, keepdims=True)
    byte = np.maximum(np.where(amax > 0, np.frexp(amax)[1] - 1 + 127, 0) - down, 1)
    scale = np.exp2(byte - 127.0)
    codes = (blocks / scale).astype(np.float32).astype(dtype).astype(np.float64)
    return np.moveaxis((codes * scale).reshape(v.shape), -1, axis)


WIDE = False


def mx_kscale(k):
    if not WIDE:
        return np.ones(k)
    levels = np.array([30, -30])
    if k % 512:
        return np.exp2(np.random.permutation(np.resize(levels, k // 32))).repeat(32)
    a = np.empty((k // 512, 16))
    for p in range(k // 512):
        a[p, :8] = np.random.permutation(np.resize(levels, 8))
        for g in range(8):
            far = levels[np.abs(levels - a[p, g]) >= 10]
            a[p, g + 8] = far[np.random.randint(len(far))]
    return np.exp2(a.ravel()).repeat(32)


BF16 = ml_dtypes.bfloat16


def bf(x):
    return np.asarray(x, np.float32).astype(BF16)


def f64(x):
    return np.asarray(x).astype(np.float64)


M, S, C = 1024, 1536, 1024


def setup_inputs():
    s = mx_kscale(S)
    t = mx_kscale(C)
    gain = (0.7 + 0.1 * np.random.standard_normal(C)) * t / s[:C]
    trim = 0.3 * np.random.standard_normal(C) * t
    limit = (0.8 + 0.1 * np.random.standard_normal(C)) * t
    return {"x": bf(np.random.standard_t(4, (M, S)) * s),
            "gain": bf(gain),
            "trim": bf(trim),
            "limit": bf(limit),
            "a": bf(np.random.standard_normal((S, S)) / np.sqrt(S) / s[:, None]),
            "b": bf(np.random.standard_normal((C, S)) / np.sqrt(C) / t[:, None])}


def reference(x, gain, trim, limit, a, b):
    xs, lim = f64(x), f64(limit)
    u = f64(trim) - xs[:, :C] * f64(gain)
    u = np.minimum(np.maximum(u, -lim), lim)
    drift = mxq(xs, 1, "e5m2") @ mxq(f64(a), 0, "e4m3")
    push = mxq(u, 1, "e4m3") @ mxq(f64(b), 0, "e4m3")
    return drift + push

@@ -1,0 +1,271 @@
+from contextlib import ExitStack
+
+import concourse.mybir as mybir
+from concourse.masks import make_identity
+
+M, S, C = 1024, 1536, 1024
+FLOPS = 2 * M * S * (S + C)
+
+F32 = mybir.dt.float32
+BF16 = mybir.dt.bfloat16
+U32 = mybir.dt.uint32
+U8 = mybir.dt.uint8
+E4M3X4 = mybir.dt.float8_e4m3fn_x4
+E5M2X4 = mybir.dt.float8_e5m2_x4
+ALU = mybir.AluOpType
+ACT = mybir.ActivationFunctionType
+
+P = 128
+PACK = 4
+K_PASS = P * PACK
+N_TILE = 512
+ROWS_HALF = 512
+ROWS_PAIR = 256
+TILES_HALF = ROWS_HALF // P
+
+X_PASSES = S // K_PASS
+U_PASSES = C // K_PASS
+PASSES = X_PASSES + U_PASSES
+SWEEPS = S // N_TILE
+HALVES = M // ROWS_HALF
+BANKS = 8
+
+
+def tile_saturated_feedback_step_s2_kernel(tc, x, gain, trim, limit, a, b, out):
+    nc = tc.nc
+
+    with ExitStack() as ctx:
+        keep = ctx.enter_context(tc.tile_pool(name="keep", bufs=1))
+        stage = ctx.enter_context(tc.tile_pool(name="stage", bufs=4))
+        psum = ctx.enter_context(tc.psum_pool(name="psum", bufs=1))
+        ctx.enter_context(tc.manual_schedule())
+
+        def weight_rows(q, cols):
+            if q < X_PASSES:
+                src = a[q * K_PASS:(q + 1) * K_PASS, cols]
+            else:
+                src = b[(q - X_PASSES) * K_PASS:(q - X_PASSES + 1) * K_PASS, cols]
+            return src.rearrange("(p j) w -> p j w", j=PACK)
+
+        raw_first = []
+        raw_rest = []
+        x_raw = []
+        for q in range(PASSES):
+            raw = keep.tile([P, PACK, N_TILE], BF16, name=f"raw_first{q}", align_bytes=64)
+            raw_first.append(raw)
+            raw = keep.tile([P, PACK, S - N_TILE], BF16, name=f"raw_rest{q}", align_bytes=64)
+            raw_rest.append(raw)
+        for pair in range(M // ROWS_PAIR):
+            raw = keep.tile([P, 2, S], BF16, name=f"x_raw{pair}", align_bytes=64)
+            x_raw.append(raw)
+
+        def load_first(q):
+            nc.sync.dma_start(out=raw_first[q][:], in_=weight_rows(q, slice(0, N_TILE)))
+
+        def load_rest(q):
+            nc.sync.dma_start(out=raw_rest[q][:], in_=weight_rows(q, slice(N_TILE, S)))
+
+        def load_x(pair):
+            rows = slice(pair * ROWS_PAIR, (pair + 1) * ROWS_PAIR)
+            nc.sync.dma_start(out=x_raw[pair][:], in_=x[rows, :].rearrange("(m p) k -> p m k", p=P))
+
+        vec_bf = {}
+        for name, vec in (("gain", gain), ("trim", trim), ("limit", limit)):
+            v = keep.tile([P, U_PASSES, PACK], BF16, name=f"{name}_bf")
+            nc.scalar.dma_start(out=v[:], in_=vec.rearrange("(g p t) -> p g t", p=P, t=PACK))
+            vec_bf[name] = v
+
+        load_first(0)
+        load_x(0)
+        load_first(1)
+        load_x(1)
+        load_first(2)
+        load_x(2)
+        load_first(3)
+        load_x(3)
+        load_first(4)
+        for q in range(PASSES):
+            load_rest(q)
+
+        ident = keep.tile([P, P], F32)
+        make_identity(nc, ident[:])
+        warm = keep.tile([P, 1], F32)
+        nc.gpsimd.memset(warm[:], 0.0)
+        warm_out = keep.tile([P, 1], F32)
+        nc.scalar.activation(out=warm_out[:], in_=warm[:], func=ACT.Identity)
+
+        def scaled_vec(name, source, factor):
+            v = keep.tile([P, U_PASSES * PACK], F32, name=name)
+            nc.gpsimd.tensor_scalar(out=v[:], in0=vec_bf[source][:].rearrange("p g t -> p (g t)"), scalar1=factor, scalar2=0.0, op0=ALU.mult, op1=ALU.add)
+            return v
+
+        neg_gain = scaled_vec("neg_gain", "gain", -1.0)
+        trim_f = scaled_vec("trim_f", "trim", 1.0)
+        lim = scaled_vec("lim", "limit", 1.0)
+        neg_lim = scaled_vec("neg_lim", "limit", -1.0)
+
+        gx, xc, xs, us, uc, usc = {}, {}, {}, {}, {}, {}
+        for h in range(HALVES):
+            for g in range(X_PASSES):
+                t = keep.tile([P, ROWS_HALF, PACK], BF16, name=f"gx{g}_{h}", align_bytes=64)
+                gx[g, h] = t
+                t = keep.tile([P, ROWS_HALF], U32, name=f"xc{g}_{h}", align_bytes=64)
+                xc[g, h] = t
+                t = keep.tile([P, ROWS_HALF], U8, name=f"xs{g}_{h}", align_bytes=64)
+                xs[g, h] = t
+            for g in range(U_PASSES):
+                t = keep.tile([P, PACK, ROWS_HALF], BF16, name=f"us{g}_{h}", align_bytes=64)
+                us[g, h] = t
+                t = keep.tile([P, ROWS_HALF], U32, name=f"uc{g}_{h}", align_bytes=64)
+                uc[g, h] = t
+                t = keep.tile([P, ROWS_HALF], U8, name=f"usc{g}_{h}", align_bytes=64)
+                usc[g, h] = t
+        wc, ws = {}, {}
+        for q in range(PASSES):
+            for n in range(SWEEPS):
+                t = keep.tile([P, N_TILE], U32, name=f"wc{q}_{n}", align_bytes=64)
+                wc[q, n] = t
+                t = keep.tile([P, N_TILE], U8, name=f"ws{q}_{n}", align_bytes=64)
+                ws[q, n] = t
+
+        t_banks = {}
+
+        def transposes(pair):
+            words = x_raw[pair][:].bitcast(F32)
+            for g in range(X_PASSES):
+                bank = psum.tile([P, 2, 2, P], F32, name=f"bank{(pair * X_PASSES + g) % BANKS}")
+                t_banks[pair, g] = bank
+                for m in range(2):
+                    for u in range(2):
+                        nc.tensor.transpose(bank[:, m, u, :], words[:, m, 256 * g + u:256 * (g + 1):2], ident[:])
+
+        def x_copies(pair):
+            h, pp = pair // 2, pair % 2
+            for g in range(X_PASSES):
+                dst = gx[g, h][:].bitcast(F32)[:, pp * ROWS_PAIR:(pp + 1) * ROWS_PAIR, :]
+                nc.scalar.copy(out=dst.rearrange("p (m r) u -> p m r u", m=2), in_=t_banks[pair, g][:].rearrange("p m u r -> p m r u"))
+
+        def x_quantize(g, h):
+            nc.vector.quantize_mx(out=xc[g, h][:].bitcast(E5M2X4), scales=xs[g, h][:], in_=gx[g, h][:].rearrange("p r t -> p (r t)"))
+
+        def affine(g, h):
+            for t in range(PACK):
+                col = slice(g * PACK + t, g * PACK + t + 1)
+                nc.scalar.activation(out=us[g, h][:, t, :], in_=gx[g, h][:, :, t], func=ACT.Identity, scale=neg_gain[:, col], bias=trim_f[:, col])
+
+        def clip(g, h):
+            for t in range(PACK):
+                col = slice(g * PACK + t, g * PACK + t + 1)
+                nc.vector.tensor_scalar(out=us[g, h][:, t, :], in0=us[g, h][:, t, :], scalar1=lim[:, col], scalar2=neg_lim[:, col], op0=ALU.min, op1=ALU.max)
+
+        def interleave(copy, dst, src):
+            copy(out=dst.rearrange("p (c i) t -> p c t i", i=4), in_=src.rearrange("p t (c i) -> p c t i", i=4))
+
+        gu = {}
+
+        def u_interleave(g, h):
+            t = stage.tile([P, ROWS_HALF, PACK], BF16, name="grouped", align_bytes=64)
+            gu[g, h] = t
+            interleave(nc.vector.tensor_copy, t[:], us[g, h][:])
+
+        def u_quantize(g, h):
+            nc.vector.quantize_mx(out=uc[g, h][:].bitcast(E4M3X4), scales=usc[g, h][:], in_=gu[g, h][:].rearrange("p r t -> p (r t)"))
+
+        gw = {}
+
+        def w_interleave(q, n, copy):
+            t = stage.tile([P, N_TILE, PACK], BF16, name="grouped", align_bytes=64)
+            gw[q, n] = t
+            src = raw_first[q][:] if n == 0 else raw_rest[q][:, :, (n - 1) * N_TILE:n * N_TILE]
+            interleave(copy, t[:], src)
+
+        def w_quantize(q, n):
+            nc.vector.quantize_mx(out=wc[q, n][:].bitcast(E4M3X4), scales=ws[q, n][:], in_=gw[q, n][:].rearrange("p r t -> p (r t)"))
+
+        acc = {}
+
+        def matmul(q, m, n):
+            h, col = m // TILES_HALF, slice((m % TILES_HALF) * P, (m % TILES_HALF + 1) * P)
+            if q == 0:
+                bank = psum.tile([P, N_TILE], F32, name=f"bank{m}")
+                acc[m] = bank
+            if q < X_PASSES:
+                codes, scales = xc[q, h][:, col].bitcast(E5M2X4), xs[q, h][:, col]
+            else:
+                codes, scales = uc[q - X_PASSES, h][:, col].bitcast(E4M3X4), usc[q - X_PASSES, h][:, col]
+            nc.tensor.matmul_mx(out=acc[m][:], lhsT=codes, lhsT_scale=scales, rhs=wc[q, n][:].bitcast(E4M3X4), rhs_scale=ws[q, n][:], start=(q == 0), stop=(q == PASSES - 1))
+
+        def evacuate(m, n, copy):
+            res = stage.tile([P, N_TILE], F32, name="res", bufs=6)
+            copy(out=res[:], in_=acc[m][:])
+            nc.sync.dma_start(out=out[m * P:(m + 1) * P, n * N_TILE:(n + 1) * N_TILE], in_=res[:])
+
+        V, A = nc.vector.tensor_copy, nc.scalar.copy
+
+        w_interleave(0, 0, V)
+        w_quantize(0, 0)
+        transposes(0)
+        x_copies(0)
+        w_interleave(1, 0, V)
+        w_quantize(1, 0)
+        transposes(1)
+        x_copies(1)
+        w_interleave(2, 0, V)
+        x_quantize(0, 0)
+        w_quantize(2, 0)
+        affine(0, 0)
+        transposes(2)
+        x_copies(2)
+        x_quantize(1, 0)
+        x_quantize(2, 0)
+        w_interleave(3, 0, V)
+        affine(1, 0)
+        transposes(3)
+        x_copies(3)
+        for q in range(X_PASSES):
+            for m in range(TILES_HALF):
+                matmul(q, m, 0)
+        clip(0, 0)
+        w_quantize(3, 0)
+        u_interleave(0, 0)
+        affine(0, 1)
+        clip(1, 0)
+        u_quantize(0, 0)
+        u_interleave(1, 0)
+        affine(1, 1)
+        w_interleave(4, 0, A)
+        x_quantize(0, 1)
+        u_quantize(1, 0)
+        x_quantize(1, 1)
+        x_quantize(2, 1)
+        for q in range(X_PASSES):
+            for m in range(TILES_HALF, 2 * TILES_HALF):
+                matmul(q, m, 0)
+        clip(0, 1)
+        u_interleave(0, 1)
+        clip(1, 1)
+        u_quantize(0, 1)
+        w_quantize(4, 0)
+        u_interleave(1, 1)
+        w_interleave(0, 1, V)
+        u_quantize(1, 1)
+
+        def close(m, n, copy):
+            for q in range(X_PASSES, PASSES):
+                matmul(q, m, n)
+            evacuate(m, n, copy)
+
+        for m in range(BANKS):
+            close(m, 0, A)
+
+        tiles = [(q, n) for n in range(1, SWEEPS) for q in range(PASSES)]
+        for i, (q, n) in enumerate(tiles):
+            if i + 1 < len(tiles):
+                w_interleave(tiles[i + 1][0], tiles[i + 1][1], V)
+            w_quantize(q, n)
+            if q < X_PASSES:
+                for m in range(BANKS):
+                    matmul(q, m, n)
+            if q == PASSES - 1:
+                for m in range(BANKS):
+                    close(m, n, V if n == SWEEPS - 1 and m % 2 else A)

@@ -18,17 +18,29 @@ ACT = mybir.ActivationFunctionType
 P = 128
 PACK = 4
 K_PASS = P * PACK
+WORDS = K_PASS // 2
 N_TILE = 512
-ROWS_HALF = 512
-ROWS_PAIR = 256
-TILES_HALF = ROWS_HALF // P
+PAIR = 2 * P
 
 X_PASSES = S // K_PASS
 U_PASSES = C // K_PASS
 PASSES = X_PASSES + U_PASSES
-SWEEPS = S // N_TILE
-HALVES = M // ROWS_HALF
+COLUMNS = S // N_TILE
+PAIRS = M // PAIR
 BANKS = 8
+
+LOADS = """
+x0 w20 w10 x1 w11 x2 w30 w01 x3 w31 w00 w21 w22 w41 w40 w42 w02 w32 w12
+"""
+
+PLAN = """
+T0 I20 C0avv F00 T1 i10 K00 Q0 F01 J00 I11 C1aaa T2 K01 S10 J01 S20 I30 F11 Q1 F10 K10 i01 S11 J10
+T3 S30 C2aaa C3vaa i00 K11 S01 I31 I21 U10 U00 F31 j11 S31 S00 I40 i41 S21 F21 S40 U11 U01 K31
+E00aa S41 Q2 E01va E10aa E11va J31 K21 Q3 F20 J21 K20 F30 U21 j20 I32 K30 U20 S32 i42 U31 J30 U30
+E20va E21aa i12 S42 i22 E30vv E31vv I02 S02 S12 S22
+"""
+HELD = 3
+TRANSPOSE_BANKS = X_PASSES
 
 
 def tile_saturated_feedback_step_s2_kernel(tc, x, gain, trim, limit, a, b, out):
@@ -40,232 +52,250 @@ def tile_saturated_feedback_step_s2_kernel(tc, x, gain, trim, limit, a, b, out):
         psum = ctx.enter_context(tc.psum_pool(name="psum", bufs=1))
         ctx.enter_context(tc.manual_schedule())
 
-        def weight_rows(q, cols):
-            if q < X_PASSES:
-                src = a[q * K_PASS:(q + 1) * K_PASS, cols]
+
+        vectors = {}
+        for name, source in (("gain", gain), ("trim", trim), ("limit", limit)):
+            tile = keep.tile([P, U_PASSES, PACK], BF16, name=f"{name}_bf16")
+            nc.scalar.dma_start(out=tile[:], in_=source.rearrange("(g p t) -> p g t", p=P, t=PACK))
+            vectors[name] = tile
+
+        x_raw = {}
+        w_raw = {}
+
+        def load_x(r):
+            for m in (2 * r, 2 * r + 1):
+                tile = keep.tile([P, S], BF16, name=f"x_raw{m}", align_bytes=64)
+                nc.sync.dma_start(out=tile[:], in_=x[m * P:(m + 1) * P, :])
+                x_raw[m] = tile
+
+        def load_weights(g, n):
+            source, row = (a, g * K_PASS) if g < X_PASSES else (b, (g - X_PASSES) * K_PASS)
+            tile = keep.tile([P, PACK, N_TILE], BF16, name=f"w_raw{g}_{n}", align_bytes=64)
+            block = source[row:row + K_PASS, n * N_TILE:(n + 1) * N_TILE]
+            nc.sync.dma_start(out=tile[:], in_=block.rearrange("(p j) w -> p j w", j=PACK))
+            w_raw[g, n] = tile
+
+        for load in LOADS.split():
+            if load[0] == "x":
+                load_x(int(load[1]))
             else:
-                src = b[(q - X_PASSES) * K_PASS:(q - X_PASSES + 1) * K_PASS, cols]
-            return src.rearrange("(p j) w -> p j w", j=PACK)
+                load_weights(int(load[1]), int(load[2]))
 
-        raw_first = []
-        raw_rest = []
-        x_raw = []
-        for q in range(PASSES):
-            raw = keep.tile([P, PACK, N_TILE], BF16, name=f"raw_first{q}", align_bytes=64)
-            raw_first.append(raw)
-            raw = keep.tile([P, PACK, S - N_TILE], BF16, name=f"raw_rest{q}", align_bytes=64)
-            raw_rest.append(raw)
-        for pair in range(M // ROWS_PAIR):
-            raw = keep.tile([P, 2, S], BF16, name=f"x_raw{pair}", align_bytes=64)
-            x_raw.append(raw)
 
-        def load_first(q):
-            nc.sync.dma_start(out=raw_first[q][:], in_=weight_rows(q, slice(0, N_TILE)))
+        identity = keep.tile([P, P], F32)
+        make_identity(nc, identity[:])
 
-        def load_rest(q):
-            nc.sync.dma_start(out=raw_rest[q][:], in_=weight_rows(q, slice(N_TILE, S)))
+        zero = keep.tile([P, 1], F32)
+        nc.gpsimd.memset(zero[:], 0.0)
+        table_load = keep.tile([P, 1], F32)
+        nc.scalar.activation(out=table_load[:], in_=zero[:], func=ACT.Identity)
 
-        def load_x(pair):
-            rows = slice(pair * ROWS_PAIR, (pair + 1) * ROWS_PAIR)
-            nc.sync.dma_start(out=x_raw[pair][:], in_=x[rows, :].rearrange("(m p) k -> p m k", p=P))
+        def scaled_vector(name, source, factor):
+            tile = keep.tile([P, U_PASSES * PACK], F32, name=name)
+            nc.gpsimd.tensor_scalar(
+                out=tile[:],
+                in0=vectors[source][:].rearrange("p g t -> p (g t)"),
+                scalar1=factor,
+                scalar2=0.0,
+                op0=ALU.mult,
+                op1=ALU.add,
+            )
+            return tile
 
-        vec_bf = {}
-        for name, vec in (("gain", gain), ("trim", trim), ("limit", limit)):
-            v = keep.tile([P, U_PASSES, PACK], BF16, name=f"{name}_bf")
-            nc.scalar.dma_start(out=v[:], in_=vec.rearrange("(g p t) -> p g t", p=P, t=PACK))
-            vec_bf[name] = v
+        minus_gain = scaled_vector("minus_gain", "gain", -1.0)
+        plus_trim = scaled_vector("plus_trim", "trim", 1.0)
+        plus_limit = scaled_vector("plus_limit", "limit", 1.0)
+        minus_limit = scaled_vector("minus_limit", "limit", -1.0)
 
-        load_first(0)
-        load_x(0)
-        load_first(1)
-        load_x(1)
-        load_first(2)
-        load_x(2)
-        load_first(3)
-        load_x(3)
-        load_first(4)
-        for q in range(PASSES):
-            load_rest(q)
 
-        ident = keep.tile([P, P], F32)
-        make_identity(nc, ident[:])
-        warm = keep.tile([P, 1], F32)
-        nc.gpsimd.memset(warm[:], 0.0)
-        warm_out = keep.tile([P, 1], F32)
-        nc.scalar.activation(out=warm_out[:], in_=warm[:], func=ACT.Identity)
+        def codes_and_scales(name, width):
+            codes = keep.tile([P, width], U32, name=f"{name}_codes", align_bytes=64)
+            scales = keep.tile([P, width], U8, name=f"{name}_scales", align_bytes=64)
+            return codes, scales
 
-        def scaled_vec(name, source, factor):
-            v = keep.tile([P, U_PASSES * PACK], F32, name=name)
-            nc.gpsimd.tensor_scalar(out=v[:], in0=vec_bf[source][:].rearrange("p g t -> p (g t)"), scalar1=factor, scalar2=0.0, op0=ALU.mult, op1=ALU.add)
-            return v
-
-        neg_gain = scaled_vec("neg_gain", "gain", -1.0)
-        trim_f = scaled_vec("trim_f", "trim", 1.0)
-        lim = scaled_vec("lim", "limit", 1.0)
-        neg_lim = scaled_vec("neg_lim", "limit", -1.0)
-
-        gx, xc, xs, us, uc, usc = {}, {}, {}, {}, {}, {}
-        for h in range(HALVES):
+        x_grouped = {}
+        u_slots = {}
+        rows_q = {}
+        for r in range(PAIRS):
+            for g in range(PASSES):
+                rows_q[g, r] = codes_and_scales(f"rows{g}_{r}", PAIR)
             for g in range(X_PASSES):
-                t = keep.tile([P, ROWS_HALF, PACK], BF16, name=f"gx{g}_{h}", align_bytes=64)
-                gx[g, h] = t
-                t = keep.tile([P, ROWS_HALF], U32, name=f"xc{g}_{h}", align_bytes=64)
-                xc[g, h] = t
-                t = keep.tile([P, ROWS_HALF], U8, name=f"xs{g}_{h}", align_bytes=64)
-                xs[g, h] = t
+                tile = keep.tile([P, PAIR, PACK], BF16, name=f"x_grouped{g}_{r}", align_bytes=64)
+                x_grouped[g, r] = tile
             for g in range(U_PASSES):
-                t = keep.tile([P, PACK, ROWS_HALF], BF16, name=f"us{g}_{h}", align_bytes=64)
-                us[g, h] = t
-                t = keep.tile([P, ROWS_HALF], U32, name=f"uc{g}_{h}", align_bytes=64)
-                uc[g, h] = t
-                t = keep.tile([P, ROWS_HALF], U8, name=f"usc{g}_{h}", align_bytes=64)
-                usc[g, h] = t
-        wc, ws = {}, {}
-        for q in range(PASSES):
-            for n in range(SWEEPS):
-                t = keep.tile([P, N_TILE], U32, name=f"wc{q}_{n}", align_bytes=64)
-                wc[q, n] = t
-                t = keep.tile([P, N_TILE], U8, name=f"ws{q}_{n}", align_bytes=64)
-                ws[q, n] = t
+                tile = keep.tile([P, PACK, PAIR], BF16, name=f"u_slots{g}_{r}", align_bytes=64)
+                u_slots[g, r] = tile
+        weights_q = {}
+        for g in range(PASSES):
+            for n in range(COLUMNS):
+                weights_q[g, n] = codes_and_scales(f"weights{g}_{n}", N_TILE)
 
-        t_banks = {}
+        free_banks = list(range(BANKS))
+        copies = {"v": nc.vector.tensor_copy, "a": nc.scalar.copy}
 
-        def transposes(pair):
-            words = x_raw[pair][:].bitcast(F32)
+
+        transposed = {}
+        pairs_transposed = []
+
+        def transpose_x(r):
             for g in range(X_PASSES):
-                bank = psum.tile([P, 2, 2, P], F32, name=f"bank{(pair * X_PASSES + g) % BANKS}")
-                t_banks[pair, g] = bank
-                for m in range(2):
+                bank = free_banks.pop(0)
+                tile = psum.tile([P, 2, 2, P], F32, name=f"bank{bank}")
+                transposed[g, r] = tile, bank
+                for i in range(2):
+                    words = x_raw[2 * r + i][:].bitcast(F32)
                     for u in range(2):
-                        nc.tensor.transpose(bank[:, m, u, :], words[:, m, 256 * g + u:256 * (g + 1):2], ident[:])
+                        nc.tensor.transpose(tile[:, i, u, :], words[:, g * WORDS + u:(g + 1) * WORDS:2], identity[:])
+            pairs_transposed.append(r)
 
-        def x_copies(pair):
-            h, pp = pair // 2, pair % 2
+        def copy_x(r, engines):
             for g in range(X_PASSES):
-                dst = gx[g, h][:].bitcast(F32)[:, pp * ROWS_PAIR:(pp + 1) * ROWS_PAIR, :]
-                nc.scalar.copy(out=dst.rearrange("p (m r) u -> p m r u", m=2), in_=t_banks[pair, g][:].rearrange("p m u r -> p m r u"))
+                tile, bank = transposed[g, r]
+                words = x_grouped[g, r][:].bitcast(F32)
+                copies[engines[g]](
+                    out=words.rearrange("p (i m) u -> p i m u", i=2),
+                    in_=tile[:].rearrange("p i u m -> p i m u"),
+                )
+                free_banks.append(bank)
 
-        def x_quantize(g, h):
-            nc.vector.quantize_mx(out=xc[g, h][:].bitcast(E5M2X4), scales=xs[g, h][:], in_=gx[g, h][:].rearrange("p r t -> p (r t)"))
+        def quantize_x(r):
+            for g in range(X_PASSES):
+                codes, scales = rows_q[g, r]
+                values = x_grouped[g, r][:].rearrange("p m t -> p (m t)")
+                nc.vector.quantize_mx(out=codes[:].bitcast(E5M2X4), scales=scales[:], in_=values)
+                ready_rows.append((g, r))
 
-        def affine(g, h):
+        def feedback(r, g):
             for t in range(PACK):
-                col = slice(g * PACK + t, g * PACK + t + 1)
-                nc.scalar.activation(out=us[g, h][:, t, :], in_=gx[g, h][:, :, t], func=ACT.Identity, scale=neg_gain[:, col], bias=trim_f[:, col])
+                column = slice(g * PACK + t, g * PACK + t + 1)
+                nc.scalar.activation(
+                    out=u_slots[g, r][:, t, :],
+                    in_=x_grouped[g, r][:, :, t],
+                    func=ACT.Identity,
+                    scale=minus_gain[:, column],
+                    bias=plus_trim[:, column],
+                )
 
-        def clip(g, h):
+        def clip(r, g):
             for t in range(PACK):
-                col = slice(g * PACK + t, g * PACK + t + 1)
-                nc.vector.tensor_scalar(out=us[g, h][:, t, :], in0=us[g, h][:, t, :], scalar1=lim[:, col], scalar2=neg_lim[:, col], op0=ALU.min, op1=ALU.max)
+                column = slice(g * PACK + t, g * PACK + t + 1)
+                nc.vector.tensor_scalar(
+                    out=u_slots[g, r][:, t, :],
+                    in0=u_slots[g, r][:, t, :],
+                    scalar1=plus_limit[:, column],
+                    scalar2=minus_limit[:, column],
+                    op0=ALU.min,
+                    op1=ALU.max,
+                )
 
-        def interleave(copy, dst, src):
-            copy(out=dst.rearrange("p (c i) t -> p c t i", i=4), in_=src.rearrange("p t (c i) -> p c t i", i=4))
+        def interleave(copy, grouped, slots):
+            copy(
+                out=grouped.rearrange("p (c i) t -> p c t i", i=4),
+                in_=slots.rearrange("p t (c i) -> p c t i", i=4),
+            )
 
-        gu = {}
+        u_grouped = {}
 
-        def u_interleave(g, h):
-            t = stage.tile([P, ROWS_HALF, PACK], BF16, name="grouped", align_bytes=64)
-            gu[g, h] = t
-            interleave(nc.vector.tensor_copy, t[:], us[g, h][:])
+        def interleave_u(copy, r, g):
+            tile = stage.tile([P, PAIR, PACK], BF16, name="u_grouped", align_bytes=64)
+            interleave(copy, tile[:], u_slots[g, r][:])
+            u_grouped[g, r] = tile
 
-        def u_quantize(g, h):
-            nc.vector.quantize_mx(out=uc[g, h][:].bitcast(E4M3X4), scales=usc[g, h][:], in_=gu[g, h][:].rearrange("p r t -> p (r t)"))
+        def quantize_u(r, g):
+            codes, scales = rows_q[X_PASSES + g, r]
+            values = u_grouped[g, r][:].rearrange("p m t -> p (m t)")
+            nc.vector.quantize_mx(out=codes[:].bitcast(E4M3X4), scales=scales[:], in_=values)
+            ready_rows.append((X_PASSES + g, r))
 
-        gw = {}
 
-        def w_interleave(q, n, copy):
-            t = stage.tile([P, N_TILE, PACK], BF16, name="grouped", align_bytes=64)
-            gw[q, n] = t
-            src = raw_first[q][:] if n == 0 else raw_rest[q][:, :, (n - 1) * N_TILE:n * N_TILE]
-            interleave(copy, t[:], src)
+        w_grouped = {}
 
-        def w_quantize(q, n):
-            nc.vector.quantize_mx(out=wc[q, n][:].bitcast(E4M3X4), scales=ws[q, n][:], in_=gw[q, n][:].rearrange("p r t -> p (r t)"))
+        def interleave_w(copy, g, n):
+            tile = stage.tile([P, N_TILE, PACK], BF16, name="w_grouped", align_bytes=64)
+            interleave(copy, tile[:], w_raw[g, n][:])
+            w_grouped[g, n] = tile
 
-        acc = {}
+        def quantize_w(g, n):
+            codes, scales = weights_q[g, n]
+            values = w_grouped[g, n][:].rearrange("p w t -> p (w t)")
+            nc.vector.quantize_mx(out=codes[:].bitcast(E4M3X4), scales=scales[:], in_=values)
+            ready_weights.append((g, n))
 
-        def matmul(q, m, n):
-            h, col = m // TILES_HALF, slice((m % TILES_HALF) * P, (m % TILES_HALF + 1) * P)
-            if q == 0:
-                bank = psum.tile([P, N_TILE], F32, name=f"bank{m}")
-                acc[m] = bank
-            if q < X_PASSES:
-                codes, scales = xc[q, h][:, col].bitcast(E5M2X4), xs[q, h][:, col]
+
+        ready_rows = []
+        ready_weights = []
+        sums = {}
+        passes_done = {}
+
+        def multiply(g, r, n):
+            done = passes_done.setdefault((r, n), [])
+            if not done:
+                sums[r, n] = []
+                for i in range(2):
+                    bank = free_banks.pop(0)
+                    tile = psum.tile([P, N_TILE], F32, name=f"bank{bank}")
+                    sums[r, n].append((tile, bank))
+            done.append(g)
+            row_codes, row_scales = rows_q[g, r]
+            w_codes, w_scales = weights_q[g, n]
+            for i in range(2):
+                rows = slice(i * P, (i + 1) * P)
+                nc.tensor.matmul_mx(
+                    out=sums[r, n][i][0][:],
+                    lhsT=row_codes[:, rows].bitcast(E5M2X4 if g < X_PASSES else E4M3X4),
+                    lhsT_scale=row_scales[:, rows],
+                    rhs=w_codes[:].bitcast(E4M3X4),
+                    rhs_scale=w_scales[:],
+                    start=len(done) == 1,
+                    stop=len(done) == PASSES,
+                )
+
+        def multiply_ready(held):
+            for n in range(COLUMNS):
+                for r in range(PAIRS):
+                    for g in range(PASSES):
+                        done = passes_done.get((r, n), [])
+                        if g in done or (g, n) in held or (g, r) not in ready_rows or (g, n) not in ready_weights:
+                            continue
+                        reserve = TRANSPOSE_BANKS if len(pairs_transposed) < PAIRS else 0
+                        if done or len(free_banks) >= 2 + reserve:
+                            multiply(g, r, n)
+
+        def store(r, n, engines):
+            for i in range(2):
+                m = 2 * r + i
+                tile, bank = sums[r, n][i]
+                result = stage.tile([P, N_TILE], F32, name="result", bufs=8)
+                copies[engines[i]](out=result[:], in_=tile[:])
+                nc.sync.dma_start(out=out[m * P:(m + 1) * P, n * N_TILE:(n + 1) * N_TILE], in_=result[:])
+                free_banks.append(bank)
+
+
+        plan = PLAN.split()
+        last = COLUMNS - 1
+        last_tiles = [(int(step[1]), last) for step in plan if step[0] == "S" and int(step[2]) == last]
+        held = last_tiles[PASSES - HELD:]
+
+        one_digit = {"T": transpose_x, "Q": quantize_x}
+        two_digits = {"F": feedback, "K": clip, "U": quantize_u, "S": quantize_w}
+        for step in plan:
+            letter, digits = step[0], [int(digit) for digit in step[1:3] if digit in "0123456789"]
+            if letter in one_digit:
+                one_digit[letter](digits[0])
+            elif letter in two_digits:
+                two_digits[letter](*digits)
+            elif letter == "C":
+                copy_x(digits[0], step[2:])
+            elif letter in "Jj":
+                interleave_u(copies["v" if letter == "J" else "a"], *digits)
+            elif letter in "Ii":
+                interleave_w(copies["v" if letter == "I" else "a"], *digits)
             else:
-                codes, scales = uc[q - X_PASSES, h][:, col].bitcast(E4M3X4), usc[q - X_PASSES, h][:, col]
-            nc.tensor.matmul_mx(out=acc[m][:], lhsT=codes, lhsT_scale=scales, rhs=wc[q, n][:].bitcast(E4M3X4), rhs_scale=ws[q, n][:], start=(q == 0), stop=(q == PASSES - 1))
+                store(*digits, step[3:])
+            multiply_ready(held)
 
-        def evacuate(m, n, copy):
-            res = stage.tile([P, N_TILE], F32, name="res", bufs=6)
-            copy(out=res[:], in_=acc[m][:])
-            nc.sync.dma_start(out=out[m * P:(m + 1) * P, n * N_TILE:(n + 1) * N_TILE], in_=res[:])
-
-        V, A = nc.vector.tensor_copy, nc.scalar.copy
-
-        w_interleave(0, 0, V)
-        w_quantize(0, 0)
-        transposes(0)
-        x_copies(0)
-        w_interleave(1, 0, V)
-        w_quantize(1, 0)
-        transposes(1)
-        x_copies(1)
-        w_interleave(2, 0, V)
-        x_quantize(0, 0)
-        w_quantize(2, 0)
-        affine(0, 0)
-        transposes(2)
-        x_copies(2)
-        x_quantize(1, 0)
-        x_quantize(2, 0)
-        w_interleave(3, 0, V)
-        affine(1, 0)
-        transposes(3)
-        x_copies(3)
-        for q in range(X_PASSES):
-            for m in range(TILES_HALF):
-                matmul(q, m, 0)
-        clip(0, 0)
-        w_quantize(3, 0)
-        u_interleave(0, 0)
-        affine(0, 1)
-        clip(1, 0)
-        u_quantize(0, 0)
-        u_interleave(1, 0)
-        affine(1, 1)
-        w_interleave(4, 0, A)
-        x_quantize(0, 1)
-        u_quantize(1, 0)
-        x_quantize(1, 1)
-        x_quantize(2, 1)
-        for q in range(X_PASSES):
-            for m in range(TILES_HALF, 2 * TILES_HALF):
-                matmul(q, m, 0)
-        clip(0, 1)
-        u_interleave(0, 1)
-        clip(1, 1)
-        u_quantize(0, 1)
-        w_quantize(4, 0)
-        u_interleave(1, 1)
-        w_interleave(0, 1, V)
-        u_quantize(1, 1)
-
-        def close(m, n, copy):
-            for q in range(X_PASSES, PASSES):
-                matmul(q, m, n)
-            evacuate(m, n, copy)
-
-        for m in range(BANKS):
-            close(m, 0, A)
-
-        tiles = [(q, n) for n in range(1, SWEEPS) for q in range(PASSES)]
-        for i, (q, n) in enumerate(tiles):
-            if i + 1 < len(tiles):
-                w_interleave(tiles[i + 1][0], tiles[i + 1][1], V)
-            w_quantize(q, n)
-            if q < X_PASSES:
-                for m in range(BANKS):
-                    matmul(q, m, n)
-            if q == PASSES - 1:
-                for m in range(BANKS):
-                    close(m, n, V if n == SWEEPS - 1 and m % 2 else A)
+        for r in range(PAIRS):
+            for g in range(PASSES):
+                if g not in passes_done.get((r, last), []):
+                    multiply(g, r, last)
+            store(r, last, "va")

@@ -28,16 +28,18 @@ PASSES = X_PASSES + U_PASSES
 COLUMNS = S // N_TILE
 PAIRS = M // PAIR
 BANKS = 8
+GAIN, TRIM, LIMIT = 0, 1, 2
+VECTORS = 3
 
 LOADS = """
-x0 w20 w10 x1 w11 x2 w30 w01 x3 w31 w00 w21 w22 w41 w40 w42 w02 w32 w12
+x0 w20 w10 x1 w40 w00 w11 x2 w30 x3 w41 w21 w01 w42 w31 w22 w02 w12 w32
 """
 
 PLAN = """
-T0 I20 C0avv F00 T1 i10 K00 Q0 F01 J00 I11 C1aaa T2 K01 S10 J01 S20 I30 F11 Q1 F10 K10 i01 S11 J10
-T3 S30 C2aaa C3vaa i00 K11 S01 I31 I21 U10 U00 F31 j11 S31 S00 I40 i41 S21 F21 S40 U11 U01 K31
-E00aa S41 Q2 E01va E10aa E11va J31 K21 Q3 F20 J21 K20 F30 U21 j20 I32 K30 U20 S32 i42 U31 J30 U30
-E20va E21aa i12 S42 i22 E30vv E31vv I02 S02 S12 S22
+I20 T0 I10 C0aaa G F00 T1 S20 Q0 S10 K00 F01 C1aaa I40 I00 Q1 T2 K01 F11 S40 S00 j00 K11 I30 F10 j01
+U01 C2aaa U00 K10 J11 T3 S30 J10 i11 U11 U10 E00aa E10aa C3aaa i31 Q2 I41 S11 F21 I21 S41 S21 F20
+F30 I01 S31 K21 S01 J21 E11aa K20 U21 Q3 F31 J20 K30 U20 E01aa K31 j31 E20aa J30 I22 U31 E21aa U30
+S22 E30aa I12 I02 E31aa S12 i42 I32 S02 S32 S42
 """
 HELD = 3
 TRANSPOSE_BANKS = X_PASSES
@@ -53,11 +55,11 @@ def tile_saturated_feedback_step_s2_kernel(tc, x, gain, trim, limit, a, b, out):
         ctx.enter_context(tc.manual_schedule())
 
 
-        vectors = {}
-        for name, source in (("gain", gain), ("trim", trim), ("limit", limit)):
-            tile = keep.tile([P, U_PASSES, PACK], BF16, name=f"{name}_bf16")
-            nc.scalar.dma_start(out=tile[:], in_=source.rearrange("(g p t) -> p g t", p=P, t=PACK))
-            vectors[name] = tile
+        vector_rows = keep.tile([P, K_PASS], BF16, name="vector_rows", align_bytes=64)
+        nc.vector.memset(vector_rows[:], 0.0)
+        for v, source in enumerate((gain, trim, limit)):
+            rows = vector_rows[v * U_PASSES:(v + 1) * U_PASSES, :]
+            nc.scalar.dma_start(out=rows, in_=source.rearrange("(g c) -> g c", g=U_PASSES))
 
         x_raw = {}
         w_raw = {}
@@ -90,22 +92,11 @@ def tile_saturated_feedback_step_s2_kernel(tc, x, gain, trim, limit, a, b, out):
         table_load = keep.tile([P, 1], F32)
         nc.scalar.activation(out=table_load[:], in_=zero[:], func=ACT.Identity)
 
-        def scaled_vector(name, source, factor):
-            tile = keep.tile([P, U_PASSES * PACK], F32, name=name)
-            nc.gpsimd.tensor_scalar(
-                out=tile[:],
-                in0=vectors[source][:].rearrange("p g t -> p (g t)"),
-                scalar1=factor,
-                scalar2=0.0,
-                op0=ALU.mult,
-                op1=ALU.add,
-            )
-            return tile
+        plus = keep.tile([P, VECTORS * U_PASSES, PACK], F32, name="plus")
+        minus = keep.tile([P, VECTORS * U_PASSES, PACK], F32, name="minus")
 
-        minus_gain = scaled_vector("minus_gain", "gain", -1.0)
-        plus_trim = scaled_vector("plus_trim", "trim", 1.0)
-        plus_limit = scaled_vector("plus_limit", "limit", 1.0)
-        minus_limit = scaled_vector("minus_limit", "limit", -1.0)
+        def vector_column(tile, v, g, t):
+            return tile[:, v * U_PASSES + g, t:t + 1]
 
 
         def codes_and_scales(name, width):
@@ -133,6 +124,25 @@ def tile_saturated_feedback_step_s2_kernel(tc, x, gain, trim, limit, a, b, out):
         free_banks = list(range(BANKS))
         copies = {"v": nc.vector.tensor_copy, "a": nc.scalar.copy}
 
+
+        def turn_vectors():
+            bank = free_banks.pop(0)
+            tile = psum.tile([P, 2, 2, P], F32, name=f"bank{bank}")
+            words = vector_rows[:].bitcast(F32)
+            for u in range(2):
+                nc.tensor.transpose(tile[:, 0, u, :], words[:, u:WORDS:2], identity[:])
+            values = tile[:, 0, :, :].bitcast(BF16)[:, :, 0:2 * VECTORS * U_PASSES]
+            values = values.rearrange("p u (c e) -> p c u e", e=2)
+            for signed, factor in ((plus, 1.0), (minus, -1.0)):
+                nc.vector.tensor_scalar(
+                    out=signed[:].rearrange("p c (u e) -> p c u e", e=2),
+                    in0=values,
+                    scalar1=factor,
+                    scalar2=0.0,
+                    op0=ALU.mult,
+                    op1=ALU.add,
+                )
+            free_banks.append(bank)
 
         transposed = {}
         pairs_transposed = []
@@ -167,23 +177,21 @@ def tile_saturated_feedback_step_s2_kernel(tc, x, gain, trim, limit, a, b, out):
 
         def feedback(r, g):
             for t in range(PACK):
-                column = slice(g * PACK + t, g * PACK + t + 1)
                 nc.scalar.activation(
                     out=u_slots[g, r][:, t, :],
                     in_=x_grouped[g, r][:, :, t],
                     func=ACT.Identity,
-                    scale=minus_gain[:, column],
-                    bias=plus_trim[:, column],
+                    scale=vector_column(minus, GAIN, g, t),
+                    bias=vector_column(plus, TRIM, g, t),
                 )
 
         def clip(r, g):
             for t in range(PACK):
-                column = slice(g * PACK + t, g * PACK + t + 1)
                 nc.vector.tensor_scalar(
                     out=u_slots[g, r][:, t, :],
                     in0=u_slots[g, r][:, t, :],
-                    scalar1=plus_limit[:, column],
-                    scalar2=minus_limit[:, column],
+                    scalar1=vector_column(plus, LIMIT, g, t),
+                    scalar2=vector_column(minus, LIMIT, g, t),
                     op0=ALU.min,
                     op1=ALU.max,
                 )
@@ -284,6 +292,8 @@ def tile_saturated_feedback_step_s2_kernel(tc, x, gain, trim, limit, a, b, out):
                 one_digit[letter](digits[0])
             elif letter in two_digits:
                 two_digits[letter](*digits)
+            elif letter == "G":
+                turn_vectors()
             elif letter == "C":
                 copy_x(digits[0], step[2:])
             elif letter in "Jj":

from contextlib import ExitStack

import concourse.mybir as mybir
from concourse.masks import make_identity

M, S, C = 1024, 1536, 1024
FLOPS = 2 * M * S * (S + C)

F32 = mybir.dt.float32
BF16 = mybir.dt.bfloat16
U32 = mybir.dt.uint32
U8 = mybir.dt.uint8
E4M3X4 = mybir.dt.float8_e4m3fn_x4
E5M2X4 = mybir.dt.float8_e5m2_x4
ALU = mybir.AluOpType
ACT = mybir.ActivationFunctionType

P = 128
PACK = 4
K_PASS = P * PACK
WORDS = K_PASS // 2
N_TILE = 512
PAIR = 2 * P

X_PASSES = S // K_PASS
U_PASSES = C // K_PASS
PASSES = X_PASSES + U_PASSES
COLUMNS = S // N_TILE
PAIRS = M // PAIR
BANKS = 8
GAIN, TRIM, LIMIT = 0, 1, 2
VECTORS = 3

LOADS = """
x0 w20 w10 x1 w40 w00 w11 x2 w30 x3 w41 w21 w01 w42 w31 w22 w02 w12 w32
"""

PLAN = """
I20 T0 I10 C0aaa G F00 T1 S20 Q0 S10 K00 F01 C1aaa I40 I00 Q1 T2 K01 F11 S40 S00 j00 K11 I30 F10 j01
U01 C2aaa U00 K10 J11 T3 S30 J10 i11 U11 U10 E00aa E10aa C3aaa i31 Q2 I41 S11 F21 I21 S41 S21 F20
F30 I01 S31 K21 S01 J21 E11aa K20 U21 Q3 F31 J20 K30 U20 E01aa K31 j31 E20aa J30 I22 U31 E21aa U30
S22 E30aa I12 I02 E31aa S12 i42 I32 S02 S32 S42
"""
HELD = 3
TRANSPOSE_BANKS = X_PASSES


def tile_saturated_feedback_step_s2_kernel(tc, x, gain, trim, limit, a, b, out):
    nc = tc.nc

    with ExitStack() as ctx:
        keep = ctx.enter_context(tc.tile_pool(name="keep", bufs=1))
        stage = ctx.enter_context(tc.tile_pool(name="stage", bufs=4))
        psum = ctx.enter_context(tc.psum_pool(name="psum", bufs=1))
        ctx.enter_context(tc.manual_schedule())


        vector_rows = keep.tile([P, K_PASS], BF16, name="vector_rows", align_bytes=64)
        nc.vector.memset(vector_rows[:], 0.0)
        for v, source in enumerate((gain, trim, limit)):
            rows = vector_rows[v * U_PASSES:(v + 1) * U_PASSES, :]
            nc.scalar.dma_start(out=rows, in_=source.rearrange("(g c) -> g c", g=U_PASSES))

        x_raw = {}
        w_raw = {}

        def load_x(r):
            for m in (2 * r, 2 * r + 1):
                tile = keep.tile([P, S], BF16, name=f"x_raw{m}", align_bytes=64)
                nc.sync.dma_start(out=tile[:], in_=x[m * P:(m + 1) * P, :])
                x_raw[m] = tile

        def load_weights(g, n):
            source, row = (a, g * K_PASS) if g < X_PASSES else (b, (g - X_PASSES) * K_PASS)
            tile = keep.tile([P, PACK, N_TILE], BF16, name=f"w_raw{g}_{n}", align_bytes=64)
            block = source[row:row + K_PASS, n * N_TILE:(n + 1) * N_TILE]
            nc.sync.dma_start(out=tile[:], in_=block.rearrange("(p j) w -> p j w", j=PACK))
            w_raw[g, n] = tile

        for load in LOADS.split():
            if load[0] == "x":
                load_x(int(load[1]))
            else:
                load_weights(int(load[1]), int(load[2]))


        identity = keep.tile([P, P], F32)
        make_identity(nc, identity[:])

        zero = keep.tile([P, 1], F32)
        nc.gpsimd.memset(zero[:], 0.0)
        table_load = keep.tile([P, 1], F32)
        nc.scalar.activation(out=table_load[:], in_=zero[:], func=ACT.Identity)

        plus = keep.tile([P, VECTORS * U_PASSES, PACK], F32, name="plus")
        minus = keep.tile([P, VECTORS * U_PASSES, PACK], F32, name="minus")

        def vector_column(tile, v, g, t):
            return tile[:, v * U_PASSES + g, t:t + 1]


        def codes_and_scales(name, width):
            codes = keep.tile([P, width], U32, name=f"{name}_codes", align_bytes=64)
            scales = keep.tile([P, width], U8, name=f"{name}_scales", align_bytes=64)
            return codes, scales

        x_grouped = {}
        u_slots = {}
        rows_q = {}
        for r in range(PAIRS):
            for g in range(PASSES):
                rows_q[g, r] = codes_and_scales(f"rows{g}_{r}", PAIR)
            for g in range(X_PASSES):
                tile = keep.tile([P, PAIR, PACK], BF16, name=f"x_grouped{g}_{r}", align_bytes=64)
                x_grouped[g, r] = tile
            for g in range(U_PASSES):
                tile = keep.tile([P, PACK, PAIR], BF16, name=f"u_slots{g}_{r}", align_bytes=64)
                u_slots[g, r] = tile
        weights_q = {}
        for g in range(PASSES):
            for n in range(COLUMNS):
                weights_q[g, n] = codes_and_scales(f"weights{g}_{n}", N_TILE)

        free_banks = list(range(BANKS))
        copies = {"v": nc.vector.tensor_copy, "a": nc.scalar.copy}


        def turn_vectors():
            bank = free_banks.pop(0)
            tile = psum.tile([P, 2, 2, P], F32, name=f"bank{bank}")
            words = vector_rows[:].bitcast(F32)
            for u in range(2):
                nc.tensor.transpose(tile[:, 0, u, :], words[:, u:WORDS:2], identity[:])
            values = tile[:, 0, :, :].bitcast(BF16)[:, :, 0:2 * VECTORS * U_PASSES]
            values = values.rearrange("p u (c e) -> p c u e", e=2)
            for signed, factor in ((plus, 1.0), (minus, -1.0)):
                nc.vector.tensor_scalar(
                    out=signed[:].rearrange("p c (u e) -> p c u e", e=2),
                    in0=values,
                    scalar1=factor,
                    scalar2=0.0,
                    op0=ALU.mult,
                    op1=ALU.add,
                )
            free_banks.append(bank)

        transposed = {}
        pairs_transposed = []

        def transpose_x(r):
            for g in range(X_PASSES):
                bank = free_banks.pop(0)
                tile = psum.tile([P, 2, 2, P], F32, name=f"bank{bank}")
                transposed[g, r] = tile, bank
                for i in range(2):
                    words = x_raw[2 * r + i][:].bitcast(F32)
                    for u in range(2):
                        nc.tensor.transpose(tile[:, i, u, :], words[:, g * WORDS + u:(g + 1) * WORDS:2], identity[:])
            pairs_transposed.append(r)

        def copy_x(r, engines):
            for g in range(X_PASSES):
                tile, bank = transposed[g, r]
                words = x_grouped[g, r][:].bitcast(F32)
                copies[engines[g]](
                    out=words.rearrange("p (i m) u -> p i m u", i=2),
                    in_=tile[:].rearrange("p i u m -> p i m u"),
                )
                free_banks.append(bank)

        def quantize_x(r):
            for g in range(X_PASSES):
                codes, scales = rows_q[g, r]
                values = x_grouped[g, r][:].rearrange("p m t -> p (m t)")
                nc.vector.quantize_mx(out=codes[:].bitcast(E5M2X4), scales=scales[:], in_=values)
                ready_rows.append((g, r))

        def feedback(r, g):
            for t in range(PACK):
                nc.scalar.activation(
                    out=u_slots[g, r][:, t, :],
                    in_=x_grouped[g, r][:, :, t],
                    func=ACT.Identity,
                    scale=vector_column(minus, GAIN, g, t),
                    bias=vector_column(plus, TRIM, g, t),
                )

        def clip(r, g):
            for t in range(PACK):
                nc.vector.tensor_scalar(
                    out=u_slots[g, r][:, t, :],
                    in0=u_slots[g, r][:, t, :],
                    scalar1=vector_column(plus, LIMIT, g, t),
                    scalar2=vector_column(minus, LIMIT, g, t),
                    op0=ALU.min,
                    op1=ALU.max,
                )

        def interleave(copy, grouped, slots):
            copy(
                out=grouped.rearrange("p (c i) t -> p c t i", i=4),
                in_=slots.rearrange("p t (c i) -> p c t i", i=4),
            )

        u_grouped = {}

        def interleave_u(copy, r, g):
            tile = stage.tile([P, PAIR, PACK], BF16, name="u_grouped", align_bytes=64)
            interleave(copy, tile[:], u_slots[g, r][:])
            u_grouped[g, r] = tile

        def quantize_u(r, g):
            codes, scales = rows_q[X_PASSES + g, r]
            values = u_grouped[g, r][:].rearrange("p m t -> p (m t)")
            nc.vector.quantize_mx(out=codes[:].bitcast(E4M3X4), scales=scales[:], in_=values)
            ready_rows.append((X_PASSES + g, r))


        w_grouped = {}

        def interleave_w(copy, g, n):
            tile = stage.tile([P, N_TILE, PACK], BF16, name="w_grouped", align_bytes=64)
            interleave(copy, tile[:], w_raw[g, n][:])
            w_grouped[g, n] = tile

        def quantize_w(g, n):
            codes, scales = weights_q[g, n]
            values = w_grouped[g, n][:].rearrange("p w t -> p (w t)")
            nc.vector.quantize_mx(out=codes[:].bitcast(E4M3X4), scales=scales[:], in_=values)
            ready_weights.append((g, n))


        ready_rows = []
        ready_weights = []
        sums = {}
        passes_done = {}

        def multiply(g, r, n):
            done = passes_done.setdefault((r, n), [])
            if not done:
                sums[r, n] = []
                for i in range(2):
                    bank = free_banks.pop(0)
                    tile = psum.tile([P, N_TILE], F32, name=f"bank{bank}")
                    sums[r, n].append((tile, bank))
            done.append(g)
            row_codes, row_scales = rows_q[g, r]
            w_codes, w_scales = weights_q[g, n]
            for i in range(2):
                rows = slice(i * P, (i + 1) * P)
                nc.tensor.matmul_mx(
                    out=sums[r, n][i][0][:],
                    lhsT=row_codes[:, rows].bitcast(E5M2X4 if g < X_PASSES else E4M3X4),
                    lhsT_scale=row_scales[:, rows],
                    rhs=w_codes[:].bitcast(E4M3X4),
                    rhs_scale=w_scales[:],
                    start=len(done) == 1,
                    stop=len(done) == PASSES,
                )

        def multiply_ready(held):
            for n in range(COLUMNS):
                for r in range(PAIRS):
                    for g in range(PASSES):
                        done = passes_done.get((r, n), [])
                        if g in done or (g, n) in held or (g, r) not in ready_rows or (g, n) not in ready_weights:
                            continue
                        reserve = TRANSPOSE_BANKS if len(pairs_transposed) < PAIRS else 0
                        if done or len(free_banks) >= 2 + reserve:
                            multiply(g, r, n)

        def store(r, n, engines):
            for i in range(2):
                m = 2 * r + i
                tile, bank = sums[r, n][i]
                result = stage.tile([P, N_TILE], F32, name="result", bufs=8)
                copies[engines[i]](out=result[:], in_=tile[:])
                nc.sync.dma_start(out=out[m * P:(m + 1) * P, n * N_TILE:(n + 1) * N_TILE], in_=result[:])
                free_banks.append(bank)


        plan = PLAN.split()
        last = COLUMNS - 1
        last_tiles = [(int(step[1]), last) for step in plan if step[0] == "S" and int(step[2]) == last]
        held = last_tiles[PASSES - HELD:]

        one_digit = {"T": transpose_x, "Q": quantize_x}
        two_digits = {"F": feedback, "K": clip, "U": quantize_u, "S": quantize_w}
        for step in plan:
            letter, digits = step[0], [int(digit) for digit in step[1:3] if digit in "0123456789"]
            if letter in one_digit:
                one_digit[letter](digits[0])
            elif letter in two_digits:
                two_digits[letter](*digits)
            elif letter == "G":
                turn_vectors()
            elif letter == "C":
                copy_x(digits[0], step[2:])
            elif letter in "Jj":
                interleave_u(copies["v" if letter == "J" else "a"], *digits)
            elif letter in "Ii":
                interleave_w(copies["v" if letter == "I" else "a"], *digits)
            else:
                store(*digits, step[3:])
            multiply_ready(held)

        for r in range(PAIRS):
            for g in range(PASSES):
                if g not in passes_done.get((r, last), []):
                    multiply(g, r, last)
            store(r, last, "va")
